import numpy as np
import ml_dtypes


def mxq(x, axis, fmt="e4m3"):
    dtype, down = {"e4m3": (ml_dtypes.float8_e4m3fn, 7), "e5m2": (ml_dtypes.float8_e5m2, 14)}[fmt]
    v = np.moveaxis(np.asarray(x, np.float32).astype(ml_dtypes.bfloat16).astype(np.float64), axis, -1)
    blocks = v.reshape(v.shape[:-1] + (-1, 32))
    amax = np.abs(blocks).max(-1, keepdims=True)
    byte = np.maximum(np.where(amax > 0, np.frexp(amax)[1] - 1 + 127, 0) - down, 1)
    scale = np.exp2(byte - 127.0)
    codes = (blocks / scale).astype(np.float32).astype(dtype).astype(np.float64)
    return np.moveaxis((codes * scale).reshape(v.shape), -1, axis)


WIDE = False


def mx_kscale(k):
    if not WIDE:
        return np.ones(k)
    levels = np.array([10, -10, 5, -5, 0])
    if k % 512:
        return np.exp2(np.random.permutation(np.resize(levels, k // 32))).repeat(32)
    a = np.empty((k // 512, 16))
    for p in range(k // 512):
        a[p, :8] = np.random.permutation(np.resize(levels, 8))
        for g in range(8):
            far = levels[np.abs(levels - a[p, g]) >= 10]
            a[p, g + 8] = far[np.random.randint(len(far))]
    return np.exp2(a.ravel()).repeat(32)


BF16 = ml_dtypes.bfloat16


def bf(x):
    return np.asarray(x, np.float32).astype(BF16)


def f64(x):
    return np.asarray(x).astype(np.float64)


E2M1 = np.array([0.0, 0.5, 1.0, 1.5, 2.0, 3.0, 4.0, 6.0, -0.0, -0.5, -1.0, -1.5, -2.0, -3.0, -4.0, -6.0])


def pack_weight(w, fmt):
    k, n = w.shape
    w = f64(bf(w)).reshape(k // 32, 32, n)
    amax = np.abs(w).max(1)
    if fmt == "e4m3":
        byte = np.frexp(amax)[1] - 1 + 127 - 7
    else:
        mant, ex = np.frexp(amax / 6.0)
        byte = np.where(mant > 0.5, ex, ex - 1) + 127
    byte = np.clip(np.where(amax > 0, byte, 1), 1, 254)
    scaled = (w * np.exp2(127.0 - byte)[:, None, :]).reshape(k, n).astype(np.float32)
    by_word = np.ascontiguousarray(scaled.reshape(k // 512, 128, 4, n).transpose(0, 1, 3, 2))
    if fmt == "e4m3":
        words = by_word.astype(ml_dtypes.float8_e4m3fn).view(np.uint8)
    else:
        c = by_word.astype(ml_dtypes.float4_e2m1fn).view(np.uint8) & 0xF
        words = c[..., 0::2] | (c[..., 1::2] << 4)
    return np.ascontiguousarray(words), np.ascontiguousarray(byte.astype(np.uint8).reshape(k // 512, 16, n))


def unpack_weight(words, scales, fmt):
    g, p, n, _ = words.shape
    if fmt == "e4m3":
        vals = np.ascontiguousarray(words).view(ml_dtypes.float8_e4m3fn).astype(np.float64)
    else:
        nib = np.empty((g, p, n, 4), np.uint8)
        nib[..., 0::2] = words & 0xF
        nib[..., 1::2] = words >> 4
        vals = E2M1[nib]
    vals = vals * np.repeat(np.exp2(scales.astype(np.float64) - 127.0), 8, axis=1)[..., None]
    return vals.transpose(0, 1, 3, 2).reshape(g * 512, n)

E4M3FN = np.array([(-1.0 if i & 128 else 1.0) * ((1.0 + (i & 7) / 8.0) * 2.0 ** (((i >> 3) & 15) - 7) if i & 120 else (i & 7) * 2.0 ** -9) for i in range(256)])


def e4m3fn_bytes(y):
    return np.clip(np.asarray(y, np.float64), -448.0, 448.0).astype(np.float32).astype(ml_dtypes.float8_e4m3fn).view(np.uint8)


def e4m3fn_values(b):
    return E4M3FN[b]


N, D, L, P = 1024, 1024, 512, 2048


def softplus(v):
    return np.maximum(v, 0.0) + np.log1p(np.exp(-np.abs(v)))


def gaussian_kl_mean(mu, lv):
    return np.mean(0.5 * (mu * mu + np.exp(lv) - 1.0 - lv), axis=-1)


def bernoulli_nll(l, x):
    return softplus(l) - x * l


def draw0():
    s, t = mx_kscale(D), mx_kscale(L)
    h = np.random.standard_normal((N, D)) * s
    wm = np.random.standard_normal((D, L)) / np.sqrt(D) / s[:, None]
    wl = (0.4 * np.random.standard_normal((D, L)) + 0.4 * np.random.standard_normal((D, 1))) / np.sqrt(D) / s[:, None]
    eps = np.random.standard_normal((N, L))
    g = (1.0 + 0.1 * np.random.standard_normal(L)) * t
    wd = np.random.standard_normal((L, P)) / np.sqrt(L) / t[:, None]
    x = np.random.uniform(0.0, 1.0, (N, P))
    wm_words, wm_scales = pack_weight(wm, "e4m3")
    wl_words, wl_scales = pack_weight(wl, "e4m3")
    wd_words, wd_scales = pack_weight(wd, "e4m3")
    return {"h": bf(h), "wm_words": wm_words, "wm_scales": wm_scales, "wl_words": wl_words, "wl_scales": wl_scales, "eps": bf(eps), "g": bf(g), "wd_words": wd_words, "wd_scales": wd_scales, "x": bf(x)}


def core(h, wm_words, wm_scales, wl_words, wl_scales, eps, g, wd_words, wd_scales, x):
    hq = mxq(f64(h), 1, "e4m3")
    mu = hq @ unpack_weight(wm_words, wm_scales, "e4m3")
    lv = hq @ unpack_weight(wl_words, wl_scales, "e4m3")
    z = mu + np.exp(0.5 * lv) * f64(eps)
    l = mxq(z * f64(g)[None, :], 1, "e4m3") @ unpack_weight(wd_words, wd_scales, "e4m3")
    rec = bernoulli_nll(l, f64(x))
    kl = gaussian_kl_mean(mu, lv)
    return rec, kl


def setup_inputs():
    drawn = draw0()
    full = np.asarray(drawn['h']).astype(np.float64)
    scale = (np.abs(full).reshape(1024, 8, 128).max(axis=(2,)) / 448.0).astype(np.float32)
    given = {}
    for key, value in drawn.items():
        if key == 'h':
            given['h_bytes'] = e4m3fn_bytes(full / np.repeat(scale.astype(np.float64), 128, axis=1))
            given['h_scale'] = scale
        else:
            given[key] = value
    return given


def reference(h_bytes, h_scale, wm_words, wm_scales, wl_words, wl_scales, eps, g, wd_words, wd_scales, x):
    return core(e4m3fn_values(h_bytes) * np.repeat(h_scale.astype(np.float64), 128, axis=1), wm_words, wm_scales, wl_words, wl_scales, eps, g, wd_words, wd_scales, x)

@@ -1,0 +1,322 @@
+from contextlib import ExitStack
+
+import concourse.mybir as mybir
+from concourse.masks import make_identity
+
+N, D, L, P_OUT = 1024, 1024, 512, 2048
+FLOPS = 2 * N * D * L * 2 + 2 * N * L * P_OUT
+
+F32 = mybir.dt.float32
+BF16 = mybir.dt.bfloat16
+U32 = mybir.dt.uint32
+I32 = mybir.dt.int32
+U8 = mybir.dt.uint8
+FP8 = mybir.dt.float8_e4m3fn
+FP8X4 = mybir.dt.float8_e4m3fn_x4
+ALU = mybir.AluOpType
+ACT = mybir.ActivationFunctionType
+AX = mybir.AxisListType
+
+P = 128
+TILES = 8
+CHUNK = 512
+LAGZ = 1
+GAIN_V = (1, 3, 5, 7)
+CLIP = 24.0
+LN_FLOOR = 2.0**-64
+
+
+def tile_gainedlatentbernoullivaeelbo_d1p_kernel(
+    tc, h_bytes, h_scale, wm_words, wm_scales, wl_words, wl_scales, eps, g, wd_words, wd_scales, x, rec, kl
+):
+    nc = tc.nc
+    with ExitStack() as ctx:
+        keep = ctx.enter_context(tc.tile_pool(name="keep", bufs=1))
+        work = ctx.enter_context(tc.tile_pool(name="work", bufs=2))
+        psum = ctx.enter_context(tc.psum_pool(name="psum", bufs=1))
+
+        ident = keep.tile([P, P], F32, name="ident")
+        wm_planes = keep.tile([P, 2, L], U8, name="wm_planes", align_bytes=64)
+        wl_planes = keep.tile([P, 2, L], U8, name="wl_planes", align_bytes=64)
+        d_planes = keep.tile([P, P_OUT], U8, name="d_planes", align_bytes=64)
+        sc = keep.tile([P, TILES, 8], F32, name="sc")
+        h_raw = keep.tile([P, TILES, D], U8, name="h_raw", align_bytes=64)
+        w_sb = {}
+        for nm in ("wm", "wl"):
+            w_sb[nm] = keep.tile([P, 2, L], U32, name=nm + "_sb", align_bytes=64)
+        wd_sb = keep.tile([P, P_OUT], U32, name="wd_sb", align_bytes=64)
+        eps_sb = keep.tile([P, TILES, L], BF16, name="eps_sb")
+        g_sb = keep.tile([P, L], BF16, name="g_sb")
+        x_sb = keep.tile([P, TILES, P_OUT], BF16, name="x_sb")
+        s_mu = keep.tile([P, TILES], F32, name="s_mu")
+        s_e = keep.tile([P, TILES], F32, name="s_e")
+        s_lv = keep.tile([P, TILES], F32, name="s_lv")
+        kl_a = keep.tile([P, TILES], F32, name="kl_a")
+        kl_b = keep.tile([P, TILES], F32, name="kl_b")
+        kl_c = keep.tile([P, TILES], F32, name="kl_c")
+
+        with tc.manual_schedule(engines={mybir.EngineType.Activation, mybir.EngineType.SP}):
+            nc.vector.memset(wm_planes[:].rearrange("p g n -> p (g n)").bitcast(I32), 0)
+            nc.vector.memset(wl_planes[:].rearrange("p g n -> p (g n)").bitcast(I32), 0)
+            nc.vector.memset(d_planes[:].bitcast(I32), 0)
+            make_identity(nc, ident[:])
+
+            h_v = h_bytes.rearrange("(p i) k -> p i k", i=TILES)
+            eps_v = eps.rearrange("(p i) n -> p i n", i=TILES)
+            x_v = x.rearrange("(p i) n -> p i n", i=TILES)
+
+            def load_words(nm, src):
+                for gg in range(2):
+                    nc.sync.dma_start(
+                        out=w_sb[nm][:, gg, :].bitcast(I32), in_=src[gg].rearrange("p n t -> p (n t)").bitcast(I32)
+                    )
+
+            def load_planes(planes, src):
+                for q in range(4):
+                    nc.sync.dma_start(
+                        out=planes[32 * q : 32 * q + 4].bitcast(I32),
+                        in_=src[:, 4 * q : 4 * q + 4, :].rearrange("g r n -> r g n").bitcast(I32),
+                    )
+
+            def load_rows(dst, src, i0, i1):
+                nc.sync.dma_start(out=dst[:, i0:i1, :], in_=src[:, i0:i1, :])
+
+            load_rows(h_raw, h_v, 0, 1)
+            nc.sync.dma_start(out=sc[:], in_=h_scale.rearrange("(p i) j -> p i j", i=TILES))
+            load_rows(h_raw, h_v, 1, 2)
+            load_words("wl", wl_words)
+            load_planes(wl_planes, wl_scales)
+            load_planes(wm_planes, wm_scales)
+            load_words("wm", wm_words)
+            load_rows(h_raw, h_v, 2, 4)
+            load_rows(eps_sb, eps_v, 0, 2)
+            nc.sync.dma_start(out=g_sb[:], in_=g.partition_broadcast(P))
+            load_rows(h_raw, h_v, 4, 8)
+            load_rows(eps_sb, eps_v, 2, 8)
+            nc.sync.dma_start(out=wd_sb[:].bitcast(I32), in_=wd_words[0].rearrange("p n t -> p (n t)").bitcast(I32))
+            for q in range(4):
+                nc.sync.dma_start(
+                    out=d_planes[32 * q : 32 * q + 4, :].bitcast(I32), in_=wd_scales[0, 4 * q : 4 * q + 4, :].bitcast(I32)
+                )
+            for i in range(TILES):
+                load_rows(x_sb, x_v, i, i + 1)
+
+            rec_v = rec.rearrange("(p i) n -> p i n", i=TILES)
+            T = {}
+
+            def widen(i, j0, j1, eng):
+                if ("hb", i) not in T:
+                    T["hb", i] = work.tile([P, D], BF16, name="hb", bufs=3, align_bytes=64)
+                for j in range(j0, j1):
+                    c = slice(128 * j, 128 * (j + 1))
+                    if eng == "v":
+                        nc.vector.tensor_scalar(
+                            out=T["hb", i][:, c], in0=h_raw[:, i, c].bitcast(FP8), scalar1=sc[:, i, j : j + 1],
+                            scalar2=None, op0=ALU.mult,
+                        )
+                    else:
+                        nc.scalar.activation(
+                            out=T["hb", i][:, c], in_=h_raw[:, i, c].bitcast(FP8), func=ACT.Copy, scale=sc[:, i, j : j + 1]
+                        )
+
+            def turn_h(i):
+                xt = psum.tile([P, 2, 2, P], F32, name="xt", bufs=2)
+                T["xt", i] = xt
+                words = T["hb", i][:].bitcast(F32)
+                for gg in range(2):
+                    for u in range(2):
+                        nc.tensor.transpose(xt[:, gg, u, :], words[:, 256 * gg + u : 256 * (gg + 1) : 2], ident[:])
+
+            def empty_h(i, eng):
+                hg = work.tile([P, 2, P, 2], F32, name="hg", bufs=3, align_bytes=64)
+                T["hg", i] = hg
+                src = T["xt", i][:].rearrange("p g u r -> p g r u")
+                if eng == "v":
+                    nc.vector.tensor_copy(out=hg[:], in_=src)
+                else:
+                    nc.scalar.copy(out=hg[:], in_=src)
+
+            def quant_h(i):
+                hq = work.tile([P, 2 * P], U32, name="hq", bufs=3, align_bytes=64)
+                hs = work.tile([P, 2 * P], U8, name="hs", bufs=3, align_bytes=64)
+                T["hq", i], T["hs", i] = hq, hs
+                nc.vector.quantize_mx(
+                    out=hq[:].bitcast(FP8X4), scales=hs[:],
+                    in_=T["hg", i][:].rearrange("p g r u -> p (g r u)").bitcast(BF16),
+                )
+
+            def pass1(out, i, nm, gg, cols, start, stop):
+                planes = {"wm": wm_planes, "wl": wl_planes}[nm]
+                nc.tensor.matmul_mx(
+                    out=out, lhsT=T["hq", i][:, P * gg : P * (gg + 1)].bitcast(FP8X4),
+                    lhsT_scale=T["hs", i][:, P * gg : P * (gg + 1)],
+                    rhs=w_sb[nm][:, gg, cols].bitcast(FP8X4), rhs_scale=planes[:, gg, cols], start=start, stop=stop,
+                )
+
+            def stage1(i):
+                lv = psum.tile([P, L], F32, name="lv", tag="acc", bufs=5)
+                mu = psum.tile([P, L], F32, name="mu", tag="acc", bufs=5)
+                T["lv", i], T["mu", i] = lv, mu
+                for nm, t in (("wl", lv), ("wm", mu)):
+                    for gg in range(2):
+                        pass1(t[:], i, nm, gg, slice(0, L), gg == 0, gg == 1)
+
+            def sum_lv(i):
+                part = psum.tile([P, L], F32, name="part", tag="acc", bufs=5)
+                T["lvs", i] = part
+                for gg in range(2):
+                    for b in range(4):
+                        pass1(part[:, 0:P], i, "wl", gg, slice(P * b, P * (b + 1)), gg + b == 0, gg + b == 4)
+
+            def red_lv(i):
+                nc.vector.tensor_reduce(out=s_lv[:, i : i + 1], in_=T["lvs", i][:, 0:P], axis=AX.X, op=ALU.add)
+
+            def std(i):
+                s = work.tile([P, L], F32, name="s", bufs=8)
+                T["s", i] = s
+                nc.scalar.activation(out=s[:], in_=T["lv", i][:], func=ACT.Exp, scale=0.5)
+
+            def sq_mu(i):
+                junk = work.tile([P, L], BF16, name="junk")
+                nc.scalar.activation(out=junk[:], in_=T["mu", i][:], func=ACT.Square, accum_out=s_mu[:, i : i + 1])
+
+            def sq_s(i):
+                junk = work.tile([P, L], BF16, name="junk")
+                nc.scalar.activation(out=junk[:], in_=T["s", i][:], func=ACT.Square, accum_out=s_e[:, i : i + 1])
+
+            def noise(i):
+                t = work.tile([P, L], F32, name="t", bufs=3)
+                T["t", i] = t
+                nc.gpsimd.tensor_tensor(out=t[:], in0=T["s", i][:], in1=eps_sb[:, i, :], op=ALU.mult)
+
+            def sample(i):
+                z = work.tile([P, L], F32, name="z", bufs=3)
+                T["z", i] = z
+                nc.vector.tensor_tensor(out=z[:], in0=T["mu", i][:], in1=T["t", i][:], op=ALU.add)
+
+            def gain(i):
+                zg = work.tile([P, L], BF16, name="zg", bufs=3, align_bytes=64)
+                T["zg", i] = zg
+                eng = nc.vector if i in GAIN_V else nc.gpsimd
+                eng.tensor_tensor(out=zg[:], in0=T["z", i][:], in1=g_sb[:], op=ALU.mult)
+
+            def turn_z(i):
+                zt = psum.tile([P, 2, P], F32, name="zt", bufs=1)
+                T["zt", i] = zt
+                words = T["zg", i][:].bitcast(F32)
+                for u in range(2):
+                    nc.tensor.transpose(zt[:, u, :], words[:, u::2], ident[:])
+
+            def empty_z(i, eng):
+                zi = work.tile([P, P, 2], F32, name="zi", bufs=3, align_bytes=64)
+                T["zi", i] = zi
+                src = T["zt", i][:].rearrange("p u r -> p r u")
+                if eng == "v":
+                    nc.vector.tensor_copy(out=zi[:], in_=src)
+                else:
+                    nc.scalar.copy(out=zi[:], in_=src)
+
+            def quant_z(i):
+                zq = work.tile([P, P], U32, name="zq", bufs=8, align_bytes=64)
+                zs = work.tile([P, P], U8, name="zs", bufs=8, align_bytes=64)
+                T["zq", i], T["zs", i] = zq, zs
+                nc.vector.quantize_mx(
+                    out=zq[:].bitcast(FP8X4), scales=zs[:], in_=T["zi", i][:].rearrange("p r u -> p (r u)").bitcast(BF16)
+                )
+
+            def stage2(i, c):
+                lo = psum.tile([P, CHUNK], F32, name="lo", tag="acc", bufs=5)
+                T["lo", i, c] = lo
+                nc.tensor.matmul_mx(
+                    out=lo[:], lhsT=T["zq", i][:].bitcast(FP8X4), lhsT_scale=T["zs", i][:],
+                    rhs=wd_sb[:, CHUNK * c : CHUNK * (c + 1)].bitcast(FP8X4), rhs_scale=d_planes[:, CHUNK * c : CHUNK * (c + 1)],
+                    start=True, stop=True,
+                )
+
+            def expo(i, c):
+                if c == 0:
+                    T["e", i] = work.tile([P, P_OUT], F32, name="e", bufs=5)
+                nc.scalar.activation(
+                    out=T["e", i][:, CHUNK * c : CHUNK * (c + 1)], in_=T["lo", i, c][:], func=ACT.Sigmoid
+                )
+
+            def x_logit(i, c):
+                xl = work.tile([P, CHUNK], F32, name="xl", bufs=3)
+                T["xl", i, c] = xl
+                nc.vector.tensor_tensor(
+                    out=xl[:], in0=T["lo", i, c][:], in1=x_sb[:, i, CHUNK * c : CHUNK * (c + 1)], op=ALU.mult
+                )
+
+            def ramp(i, c):
+                if c == 0:
+                    T["r", i] = work.tile([P, P_OUT], F32, name="r", bufs=5)
+                nc.vector.scalar_tensor_tensor(
+                    out=T["r", i][:, CHUNK * c : CHUNK * (c + 1)], in0=T["lo", i, c][:], scalar=-CLIP, in1=T["xl", i, c][:],
+                    op0=ALU.max, op1=ALU.subtract,
+                )
+
+            def log(i, c0, c1):
+                e = T["e", i][:, c0:c1]
+                nc.scalar.activation(out=e, in_=e, func=ACT.Ln, bias=LN_FLOOR)
+
+            def total(i, c0, c1):
+                r = T["r", i][:, c0:c1]
+                nc.vector.scalar_tensor_tensor(
+                    out=r, in0=T["e", i][:, c0:c1], scalar=-CLIP, in1=r, op0=ALU.max, op1=ALU.subtract, reverse1=True
+                )
+                nc.sync.dma_start(out=rec_v[:, i, c0:c1], in_=r)
+
+            def in_range(i):
+                return 0 <= i < TILES
+
+            def head(n):
+                if in_range(n + 1):
+                    std(n + 1)
+                    noise(n + 1)
+                    sq_mu(n + 1)
+                    sum_lv(n + 1)
+                if in_range(n + 3):
+                    turn_h(n + 3)
+                    empty_h(n + 3, "s")
+                if in_range(n):
+                    turn_z(n)
+                if in_range(n - LAGZ):
+                    empty_z(n - LAGZ, "s")
+                    quant_z(n - LAGZ)
+                if in_range(n + 2):
+                    quant_h(n + 2)
+                    stage1(n + 2)
+                if in_range(n + 1):
+                    sample(n + 1)
+                    gain(n + 1)
+                    red_lv(n + 1)
+                if in_range(n + 4):
+                    widen(n + 4, 0, 8, "v")
+
+            for n in range(-4, TILES + LAGZ):
+                head(n)
+
+            batches = {4: (0, 1, 2, 3), 7: (4, 5, 6, 7)}
+            for i in range(TILES):
+                for c in range(4):
+                    stage2(i, c)
+                    if i == 0:
+                        x_logit(i, c)
+                    expo(i, c)
+                    if i:
+                        x_logit(i, c)
+                    if c:
+                        ramp(i, c - 1)
+                ramp(i, 3)
+                sq_s(i)
+                for b in batches.get(i, ()):
+                    for c0 in (0, 1024):
+                        log(b, c0, c0 + 1024)
+                        total(b, c0, c0 + 1024)
+
+            nc.vector.tensor_tensor(out=kl_a[:], in0=s_mu[:], in1=s_e[:], op=ALU.add)
+            nc.vector.tensor_tensor(out=kl_b[:], in0=kl_a[:], in1=s_lv[:], op=ALU.subtract)
+            nc.vector.tensor_scalar(
+                out=kl_c[:], in0=kl_b[:], scalar1=0.5 / L, scalar2=-0.5, op0=ALU.mult, op1=ALU.add
+            )
+            nc.sync.dma_start(out=kl.rearrange("(p i) -> p i", i=TILES), in_=kl_c[:])

@@ -20,8 +20,13 @@ AX = mybir.AxisListType
 P = 128
 TILES = 8
 CHUNK = 512
-LAGZ = 1
-GAIN_V = (1, 3, 5, 7)
+NOISE_V = (0,)
+G_TILES = ()
+BATCHES = {4: (0, 1, 2, 3), 7: (4, 5, 6, 7)}
+SQ_V = ()
+EB, RB = 6, 6
+GAIN_V = (0,)
+TB = 3
 CLIP = 24.0
 LN_FLOOR = 2.0**-64
 
@@ -83,15 +88,15 @@ def tile_gainedlatentbernoullivaeelbo_d1p_kernel(
 
             load_rows(h_raw, h_v, 0, 1)
             nc.sync.dma_start(out=sc[:], in_=h_scale.rearrange("(p i) j -> p i j", i=TILES))
-            load_rows(h_raw, h_v, 1, 2)
-            load_words("wl", wl_words)
             load_planes(wl_planes, wl_scales)
+            load_words("wl", wl_words)
+            load_rows(h_raw, h_v, 1, 2)
+            load_rows(h_raw, h_v, 2, 5)
+            load_rows(eps_sb, eps_v, 0, 2)
             load_planes(wm_planes, wm_scales)
             load_words("wm", wm_words)
-            load_rows(h_raw, h_v, 2, 4)
-            load_rows(eps_sb, eps_v, 0, 2)
+            load_rows(h_raw, h_v, 5, 8)
             nc.sync.dma_start(out=g_sb[:], in_=g.partition_broadcast(P))
-            load_rows(h_raw, h_v, 4, 8)
             load_rows(eps_sb, eps_v, 2, 8)
             nc.sync.dma_start(out=wd_sb[:].bitcast(I32), in_=wd_words[0].rearrange("p n t -> p (n t)").bitcast(I32))
             for q in range(4):
@@ -120,7 +125,7 @@ def tile_gainedlatentbernoullivaeelbo_d1p_kernel(
                         )
 
             def turn_h(i):
-                xt = psum.tile([P, 2, 2, P], F32, name="xt", bufs=2)
+                xt = psum.tile([P, 2, 2, P], F32, name="xt", tag="turn", bufs=2)
                 T["xt", i] = xt
                 words = T["hb", i][:].bitcast(F32)
                 for gg in range(2):
@@ -137,8 +142,8 @@ def tile_gainedlatentbernoullivaeelbo_d1p_kernel(
                     nc.scalar.copy(out=hg[:], in_=src)
 
             def quant_h(i):
-                hq = work.tile([P, 2 * P], U32, name="hq", bufs=3, align_bytes=64)
-                hs = work.tile([P, 2 * P], U8, name="hs", bufs=3, align_bytes=64)
+                hq = work.tile([P, 2 * P], U32, name="hq", bufs=8, align_bytes=64)
+                hs = work.tile([P, 2 * P], U8, name="hs", bufs=8, align_bytes=64)
                 T["hq", i], T["hs", i] = hq, hs
                 nc.vector.quantize_mx(
                     out=hq[:].bitcast(FP8X4), scales=hs[:],
@@ -153,13 +158,11 @@ def tile_gainedlatentbernoullivaeelbo_d1p_kernel(
                     rhs=w_sb[nm][:, gg, cols].bitcast(FP8X4), rhs_scale=planes[:, gg, cols], start=start, stop=stop,
                 )
 
-            def stage1(i):
-                lv = psum.tile([P, L], F32, name="lv", tag="acc", bufs=5)
-                mu = psum.tile([P, L], F32, name="mu", tag="acc", bufs=5)
-                T["lv", i], T["mu", i] = lv, mu
-                for nm, t in (("wl", lv), ("wm", mu)):
-                    for gg in range(2):
-                        pass1(t[:], i, nm, gg, slice(0, L), gg == 0, gg == 1)
+            def stage1(i, nm, tag, bufs):
+                t = psum.tile([P, L], F32, name=nm + "_acc", tag=tag, bufs=bufs)
+                T[{"wl": "lv", "wm": "mu"}[nm], i] = t
+                for gg in range(2):
+                    pass1(t[:], i, nm, gg, slice(0, L), gg == 0, gg == 1)
 
             def sum_lv(i):
                 part = psum.tile([P, L], F32, name="part", tag="acc", bufs=5)
@@ -182,12 +185,19 @@ def tile_gainedlatentbernoullivaeelbo_d1p_kernel(
 
             def sq_s(i):
                 junk = work.tile([P, L], BF16, name="junk")
-                nc.scalar.activation(out=junk[:], in_=T["s", i][:], func=ACT.Square, accum_out=s_e[:, i : i + 1])
+                if i in SQ_V:
+                    nc.vector.scalar_tensor_tensor(
+                        out=junk[:], in0=T["s", i][:], scalar=1.0, in1=T["s", i][:], op0=ALU.mult, op1=ALU.mult,
+                        accum_out=s_e[:, i : i + 1],
+                    )
+                else:
+                    nc.scalar.activation(out=junk[:], in_=T["s", i][:], func=ACT.Square, accum_out=s_e[:, i : i + 1])
 
             def noise(i):
-                t = work.tile([P, L], F32, name="t", bufs=3)
+                t = work.tile([P, L], F32, name="t", bufs=TB)
                 T["t", i] = t
-                nc.gpsimd.tensor_tensor(out=t[:], in0=T["s", i][:], in1=eps_sb[:, i, :], op=ALU.mult)
+                eng = nc.vector if i in NOISE_V else nc.gpsimd
+                eng.tensor_tensor(out=t[:], in0=T["s", i][:], in1=eps_sb[:, i, :], op=ALU.mult)
 
             def sample(i):
                 z = work.tile([P, L], F32, name="z", bufs=3)
@@ -201,7 +211,7 @@ def tile_gainedlatentbernoullivaeelbo_d1p_kernel(
                 eng.tensor_tensor(out=zg[:], in0=T["z", i][:], in1=g_sb[:], op=ALU.mult)
 
             def turn_z(i):
-                zt = psum.tile([P, 2, P], F32, name="zt", bufs=1)
+                zt = psum.tile([P, 2, P], F32, name="zt", tag="turn", bufs=2)
                 T["zt", i] = zt
                 words = T["zg", i][:].bitcast(F32)
                 for u in range(2):
@@ -235,7 +245,7 @@ def tile_gainedlatentbernoullivaeelbo_d1p_kernel(
 
             def expo(i, c):
                 if c == 0:
-                    T["e", i] = work.tile([P, P_OUT], F32, name="e", bufs=5)
+                    T["e", i] = work.tile([P, P_OUT], F32, name="e", bufs=EB)
                 nc.scalar.activation(
                     out=T["e", i][:, CHUNK * c : CHUNK * (c + 1)], in_=T["lo", i, c][:], func=ACT.Sigmoid
                 )
@@ -249,11 +259,38 @@ def tile_gainedlatentbernoullivaeelbo_d1p_kernel(
 
             def ramp(i, c):
                 if c == 0:
-                    T["r", i] = work.tile([P, P_OUT], F32, name="r", bufs=5)
+                    T["r", i] = work.tile([P, P_OUT], F32, name="r", bufs=RB)
                 nc.vector.scalar_tensor_tensor(
                     out=T["r", i][:, CHUNK * c : CHUNK * (c + 1)], in0=T["lo", i, c][:], scalar=-CLIP, in1=T["xl", i, c][:],
                     op0=ALU.max, op1=ALU.subtract,
                 )
+
+            def floor_logit(i, c):
+                if c == 0:
+                    T["a", i] = work.tile([P, P_OUT], F32, name="a", bufs=3)
+                nc.vector.tensor_scalar(
+                    out=T["a", i][:, CHUNK * c : CHUNK * (c + 1)], in0=T["lo", i, c][:], scalar1=-CLIP, scalar2=None, op0=ALU.max
+                )
+
+            def x_logit_wide(i, c):
+                if c == 0:
+                    T["r", i] = work.tile([P, P_OUT], F32, name="r", bufs=RB)
+                cs = slice(CHUNK * c, CHUNK * (c + 1))
+                nc.vector.tensor_tensor(out=T["r", i][:, cs], in0=T["lo", i, c][:], in1=x_sb[:, i, cs], op=ALU.mult)
+
+            def expo_wide(i, c0, c1):
+                if c0 == 0:
+                    T["e", i] = work.tile([P, P_OUT], F32, name="e", bufs=EB)
+                nc.scalar.activation(out=T["e", i][:, c0:c1], in_=T["a", i][:, c0:c1], func=ACT.Sigmoid)
+
+            def ramp_wide(i, c0, c1):
+                r = T["r", i][:, c0:c1]
+                nc.gpsimd.tensor_tensor(out=r, in0=T["a", i][:, c0:c1], in1=r, op=ALU.subtract)
+
+            def total_wide(i, c0, c1):
+                r = T["r", i][:, c0:c1]
+                nc.gpsimd.tensor_tensor(out=r, in0=r, in1=T["e", i][:, c0:c1], op=ALU.subtract)
+                nc.sync.dma_start(out=rec_v[:, i, c0:c1], in_=r)
 
             def log(i, c0, c1):
                 e = T["e", i][:, c0:c1]
@@ -269,50 +306,61 @@ def tile_gainedlatentbernoullivaeelbo_d1p_kernel(
             def in_range(i):
                 return 0 <= i < TILES
 
+            def z_begin(i):
+                stage1(i, "wm", "mu", 1)
+                sq_mu(i)
+                noise(i)
+                sample(i)
+                gain(i)
+
+            def z_end(i):
+                turn_z(i)
+                empty_z(i, "s")
+                quant_z(i)
+
             def head(n):
-                if in_range(n + 1):
-                    std(n + 1)
-                    noise(n + 1)
-                    sq_mu(n + 1)
-                    sum_lv(n + 1)
-                if in_range(n + 3):
-                    turn_h(n + 3)
-                    empty_h(n + 3, "s")
                 if in_range(n):
-                    turn_z(n)
-                if in_range(n - LAGZ):
-                    empty_z(n - LAGZ, "s")
-                    quant_z(n - LAGZ)
+                    std(n)
+                    sum_lv(n)
                 if in_range(n + 2):
-                    quant_h(n + 2)
-                    stage1(n + 2)
+                    turn_h(n + 2)
+                    empty_h(n + 2, "s")
                 if in_range(n + 1):
-                    sample(n + 1)
-                    gain(n + 1)
-                    red_lv(n + 1)
-                if in_range(n + 4):
-                    widen(n + 4, 0, 8, "v")
+                    quant_h(n + 1)
+                    stage1(n + 1, "wl", "acc", 5)
+                if in_range(n):
+                    red_lv(n)
+                if n in {2: 0, 4: 1}:
+                    z_begin({2: 0, 4: 1}[n])
+                if n - 1 in {2: 0, 4: 1}:
+                    z_end({2: 0, 4: 1}[n - 1])
+                if in_range(n + 3):
+                    widen(n + 3, 0, 8, "v")
 
-            for n in range(-4, TILES + LAGZ):
+            for n in range(-3, TILES):
                 head(n)
+            if TILES - 1 in {2: 0, 4: 1}:
+                z_end({2: 0, 4: 1}[TILES - 1])
 
-            batches = {4: (0, 1, 2, 3), 7: (4, 5, 6, 7)}
+            warm = keep.tile([P, 1], F32, name="warm")
+            nc.scalar.activation(out=warm[:], in_=s_lv[:, 0:1], func=ACT.Sigmoid)
             for i in range(TILES):
                 for c in range(4):
                     stage2(i, c)
-                    if i == 0:
-                        x_logit(i, c)
                     expo(i, c)
-                    if i:
-                        x_logit(i, c)
+                    x_logit(i, c)
                     if c:
                         ramp(i, c - 1)
+                    if c == 0 and in_range(i + 2):
+                        z_begin(i + 2)
                 ramp(i, 3)
-                sq_s(i)
-                for b in batches.get(i, ()):
+                for b in BATCHES.get(i, ()):
                     for c0 in (0, 1024):
                         log(b, c0, c0 + 1024)
                         total(b, c0, c0 + 1024)
+                if in_range(i + 2):
+                    z_end(i + 2)
+                sq_s(i)
 
             nc.vector.tensor_tensor(out=kl_a[:], in0=s_mu[:], in1=s_e[:], op=ALU.add)
             nc.vector.tensor_tensor(out=kl_b[:], in0=kl_a[:], in1=s_lv[:], op=ALU.subtract)

from contextlib import ExitStack

import concourse.mybir as mybir
from concourse.masks import make_identity

N, D, L, P_OUT = 1024, 1024, 512, 2048
FLOPS = 2 * N * D * L * 2 + 2 * N * L * P_OUT

F32 = mybir.dt.float32
BF16 = mybir.dt.bfloat16
U32 = mybir.dt.uint32
I32 = mybir.dt.int32
U8 = mybir.dt.uint8
FP8 = mybir.dt.float8_e4m3fn
FP8X4 = mybir.dt.float8_e4m3fn_x4
ALU = mybir.AluOpType
ACT = mybir.ActivationFunctionType
AX = mybir.AxisListType

P = 128
TILES = 8
CHUNK = 512
NOISE_V = (0,)
G_TILES = ()
BATCHES = {4: (0, 1, 2, 3), 7: (4, 5, 6, 7)}
SQ_V = ()
EB, RB = 6, 6
GAIN_V = (0,)
TB = 3
CLIP = 24.0
LN_FLOOR = 2.0**-64


def tile_gainedlatentbernoullivaeelbo_d1p_kernel(
    tc, h_bytes, h_scale, wm_words, wm_scales, wl_words, wl_scales, eps, g, wd_words, wd_scales, x, rec, kl
):
    nc = tc.nc
    with ExitStack() as ctx:
        keep = ctx.enter_context(tc.tile_pool(name="keep", bufs=1))
        work = ctx.enter_context(tc.tile_pool(name="work", bufs=2))
        psum = ctx.enter_context(tc.psum_pool(name="psum", bufs=1))

        ident = keep.tile([P, P], F32, name="ident")
        wm_planes = keep.tile([P, 2, L], U8, name="wm_planes", align_bytes=64)
        wl_planes = keep.tile([P, 2, L], U8, name="wl_planes", align_bytes=64)
        d_planes = keep.tile([P, P_OUT], U8, name="d_planes", align_bytes=64)
        sc = keep.tile([P, TILES, 8], F32, name="sc")
        h_raw = keep.tile([P, TILES, D], U8, name="h_raw", align_bytes=64)
        w_sb = {}
        for nm in ("wm", "wl"):
            w_sb[nm] = keep.tile([P, 2, L], U32, name=nm + "_sb", align_bytes=64)
        wd_sb = keep.tile([P, P_OUT], U32, name="wd_sb", align_bytes=64)
        eps_sb = keep.tile([P, TILES, L], BF16, name="eps_sb")
        g_sb = keep.tile([P, L], BF16, name="g_sb")
        x_sb = keep.tile([P, TILES, P_OUT], BF16, name="x_sb")
        s_mu = keep.tile([P, TILES], F32, name="s_mu")
        s_e = keep.tile([P, TILES], F32, name="s_e")
        s_lv = keep.tile([P, TILES], F32, name="s_lv")
        kl_a = keep.tile([P, TILES], F32, name="kl_a")
        kl_b = keep.tile([P, TILES], F32, name="kl_b")
        kl_c = keep.tile([P, TILES], F32, name="kl_c")

        with tc.manual_schedule(engines={mybir.EngineType.Activation, mybir.EngineType.SP}):
            nc.vector.memset(wm_planes[:].rearrange("p g n -> p (g n)").bitcast(I32), 0)
            nc.vector.memset(wl_planes[:].rearrange("p g n -> p (g n)").bitcast(I32), 0)
            nc.vector.memset(d_planes[:].bitcast(I32), 0)
            make_identity(nc, ident[:])

            h_v = h_bytes.rearrange("(p i) k -> p i k", i=TILES)
            eps_v = eps.rearrange("(p i) n -> p i n", i=TILES)
            x_v = x.rearrange("(p i) n -> p i n", i=TILES)

            def load_words(nm, src):
                for gg in range(2):
                    nc.sync.dma_start(
                        out=w_sb[nm][:, gg, :].bitcast(I32), in_=src[gg].rearrange("p n t -> p (n t)").bitcast(I32)
                    )

            def load_planes(planes, src):
                for q in range(4):
                    nc.sync.dma_start(
                        out=planes[32 * q : 32 * q + 4].bitcast(I32),
                        in_=src[:, 4 * q : 4 * q + 4, :].rearrange("g r n -> r g n").bitcast(I32),
                    )

            def load_rows(dst, src, i0, i1):
                nc.sync.dma_start(out=dst[:, i0:i1, :], in_=src[:, i0:i1, :])

            load_rows(h_raw, h_v, 0, 1)
            nc.sync.dma_start(out=sc[:], in_=h_scale.rearrange("(p i) j -> p i j", i=TILES))
            load_planes(wl_planes, wl_scales)
            load_words("wl", wl_words)
            load_rows(h_raw, h_v, 1, 2)
            load_rows(h_raw, h_v, 2, 5)
            load_rows(eps_sb, eps_v, 0, 2)
            load_planes(wm_planes, wm_scales)
            load_words("wm", wm_words)
            load_rows(h_raw, h_v, 5, 8)
            nc.sync.dma_start(out=g_sb[:], in_=g.partition_broadcast(P))
            load_rows(eps_sb, eps_v, 2, 8)
            nc.sync.dma_start(out=wd_sb[:].bitcast(I32), in_=wd_words[0].rearrange("p n t -> p (n t)").bitcast(I32))
            for q in range(4):
                nc.sync.dma_start(
                    out=d_planes[32 * q : 32 * q + 4, :].bitcast(I32), in_=wd_scales[0, 4 * q : 4 * q + 4, :].bitcast(I32)
                )
            for i in range(TILES):
                load_rows(x_sb, x_v, i, i + 1)

            rec_v = rec.rearrange("(p i) n -> p i n", i=TILES)
            T = {}

            def widen(i, j0, j1, eng):
                if ("hb", i) not in T:
                    T["hb", i] = work.tile([P, D], BF16, name="hb", bufs=3, align_bytes=64)
                for j in range(j0, j1):
                    c = slice(128 * j, 128 * (j + 1))
                    if eng == "v":
                        nc.vector.tensor_scalar(
                            out=T["hb", i][:, c], in0=h_raw[:, i, c].bitcast(FP8), scalar1=sc[:, i, j : j + 1],
                            scalar2=None, op0=ALU.mult,
                        )
                    else:
                        nc.scalar.activation(
                            out=T["hb", i][:, c], in_=h_raw[:, i, c].bitcast(FP8), func=ACT.Copy, scale=sc[:, i, j : j + 1]
                        )

            def turn_h(i):
                xt = psum.tile([P, 2, 2, P], F32, name="xt", tag="turn", bufs=2)
                T["xt", i] = xt
                words = T["hb", i][:].bitcast(F32)
                for gg in range(2):
                    for u in range(2):
                        nc.tensor.transpose(xt[:, gg, u, :], words[:, 256 * gg + u : 256 * (gg + 1) : 2], ident[:])

            def empty_h(i, eng):
                hg = work.tile([P, 2, P, 2], F32, name="hg", bufs=3, align_bytes=64)
                T["hg", i] = hg
                src = T["xt", i][:].rearrange("p g u r -> p g r u")
                if eng == "v":
                    nc.vector.tensor_copy(out=hg[:], in_=src)
                else:
                    nc.scalar.copy(out=hg[:], in_=src)

            def quant_h(i):
                hq = work.tile([P, 2 * P], U32, name="hq", bufs=8, align_bytes=64)
                hs = work.tile([P, 2 * P], U8, name="hs", bufs=8, align_bytes=64)
                T["hq", i], T["hs", i] = hq, hs
                nc.vector.quantize_mx(
                    out=hq[:].bitcast(FP8X4), scales=hs[:],
                    in_=T["hg", i][:].rearrange("p g r u -> p (g r u)").bitcast(BF16),
                )

            def pass1(out, i, nm, gg, cols, start, stop):
                planes = {"wm": wm_planes, "wl": wl_planes}[nm]
                nc.tensor.matmul_mx(
                    out=out, lhsT=T["hq", i][:, P * gg : P * (gg + 1)].bitcast(FP8X4),
                    lhsT_scale=T["hs", i][:, P * gg : P * (gg + 1)],
                    rhs=w_sb[nm][:, gg, cols].bitcast(FP8X4), rhs_scale=planes[:, gg, cols], start=start, stop=stop,
                )

            def stage1(i, nm, tag, bufs):
                t = psum.tile([P, L], F32, name=nm + "_acc", tag=tag, bufs=bufs)
                T[{"wl": "lv", "wm": "mu"}[nm], i] = t
                for gg in range(2):
                    pass1(t[:], i, nm, gg, slice(0, L), gg == 0, gg == 1)

            def sum_lv(i):
                part = psum.tile([P, L], F32, name="part", tag="acc", bufs=5)
                T["lvs", i] = part
                for gg in range(2):
                    for b in range(4):
                        pass1(part[:, 0:P], i, "wl", gg, slice(P * b, P * (b + 1)), gg + b == 0, gg + b == 4)

            def red_lv(i):
                nc.vector.tensor_reduce(out=s_lv[:, i : i + 1], in_=T["lvs", i][:, 0:P], axis=AX.X, op=ALU.add)

            def std(i):
                s = work.tile([P, L], F32, name="s", bufs=8)
                T["s", i] = s
                nc.scalar.activation(out=s[:], in_=T["lv", i][:], func=ACT.Exp, scale=0.5)

            def sq_mu(i):
                junk = work.tile([P, L], BF16, name="junk")
                nc.scalar.activation(out=junk[:], in_=T["mu", i][:], func=ACT.Square, accum_out=s_mu[:, i : i + 1])

            def sq_s(i):
                junk = work.tile([P, L], BF16, name="junk")
                if i in SQ_V:
                    nc.vector.scalar_tensor_tensor(
                        out=junk[:], in0=T["s", i][:], scalar=1.0, in1=T["s", i][:], op0=ALU.mult, op1=ALU.mult,
                        accum_out=s_e[:, i : i + 1],
                    )
                else:
                    nc.scalar.activation(out=junk[:], in_=T["s", i][:], func=ACT.Square, accum_out=s_e[:, i : i + 1])

            def noise(i):
                t = work.tile([P, L], F32, name="t", bufs=TB)
                T["t", i] = t
                eng = nc.vector if i in NOISE_V else nc.gpsimd
                eng.tensor_tensor(out=t[:], in0=T["s", i][:], in1=eps_sb[:, i, :], op=ALU.mult)

            def sample(i):
                z = work.tile([P, L], F32, name="z", bufs=3)
                T["z", i] = z
                nc.vector.tensor_tensor(out=z[:], in0=T["mu", i][:], in1=T["t", i][:], op=ALU.add)

            def gain(i):
                zg = work.tile([P, L], BF16, name="zg", bufs=3, align_bytes=64)
                T["zg", i] = zg
                eng = nc.vector if i in GAIN_V else nc.gpsimd
                eng.tensor_tensor(out=zg[:], in0=T["z", i][:], in1=g_sb[:], op=ALU.mult)

            def turn_z(i):
                zt = psum.tile([P, 2, P], F32, name="zt", tag="turn", bufs=2)
                T["zt", i] = zt
                words = T["zg", i][:].bitcast(F32)
                for u in range(2):
                    nc.tensor.transpose(zt[:, u, :], words[:, u::2], ident[:])

            def empty_z(i, eng):
                zi = work.tile([P, P, 2], F32, name="zi", bufs=3, align_bytes=64)
                T["zi", i] = zi
                src = T["zt", i][:].rearrange("p u r -> p r u")
                if eng == "v":
                    nc.vector.tensor_copy(out=zi[:], in_=src)
                else:
                    nc.scalar.copy(out=zi[:], in_=src)

            def quant_z(i):
                zq = work.tile([P, P], U32, name="zq", bufs=8, align_bytes=64)
                zs = work.tile([P, P], U8, name="zs", bufs=8, align_bytes=64)
                T["zq", i], T["zs", i] = zq, zs
                nc.vector.quantize_mx(
                    out=zq[:].bitcast(FP8X4), scales=zs[:], in_=T["zi", i][:].rearrange("p r u -> p (r u)").bitcast(BF16)
                )

            def stage2(i, c):
                lo = psum.tile([P, CHUNK], F32, name="lo", tag="acc", bufs=5)
                T["lo", i, c] = lo
                nc.tensor.matmul_mx(
                    out=lo[:], lhsT=T["zq", i][:].bitcast(FP8X4), lhsT_scale=T["zs", i][:],
                    rhs=wd_sb[:, CHUNK * c : CHUNK * (c + 1)].bitcast(FP8X4), rhs_scale=d_planes[:, CHUNK * c : CHUNK * (c + 1)],
                    start=True, stop=True,
                )

            def expo(i, c):
                if c == 0:
                    T["e", i] = work.tile([P, P_OUT], F32, name="e", bufs=EB)
                nc.scalar.activation(
                    out=T["e", i][:, CHUNK * c : CHUNK * (c + 1)], in_=T["lo", i, c][:], func=ACT.Sigmoid
                )

            def x_logit(i, c):
                xl = work.tile([P, CHUNK], F32, name="xl", bufs=3)
                T["xl", i, c] = xl
                nc.vector.tensor_tensor(
                    out=xl[:], in0=T["lo", i, c][:], in1=x_sb[:, i, CHUNK * c : CHUNK * (c + 1)], op=ALU.mult
                )

            def ramp(i, c):
                if c == 0:
                    T["r", i] = work.tile([P, P_OUT], F32, name="r", bufs=RB)
                nc.vector.scalar_tensor_tensor(
                    out=T["r", i][:, CHUNK * c : CHUNK * (c + 1)], in0=T["lo", i, c][:], scalar=-CLIP, in1=T["xl", i, c][:],
                    op0=ALU.max, op1=ALU.subtract,
                )

            def floor_logit(i, c):
                if c == 0:
                    T["a", i] = work.tile([P, P_OUT], F32, name="a", bufs=3)
                nc.vector.tensor_scalar(
                    out=T["a", i][:, CHUNK * c : CHUNK * (c + 1)], in0=T["lo", i, c][:], scalar1=-CLIP, scalar2=None, op0=ALU.max
                )

            def x_logit_wide(i, c):
                if c == 0:
                    T["r", i] = work.tile([P, P_OUT], F32, name="r", bufs=RB)
                cs = slice(CHUNK * c, CHUNK * (c + 1))
                nc.vector.tensor_tensor(out=T["r", i][:, cs], in0=T["lo", i, c][:], in1=x_sb[:, i, cs], op=ALU.mult)

            def expo_wide(i, c0, c1):
                if c0 == 0:
                    T["e", i] = work.tile([P, P_OUT], F32, name="e", bufs=EB)
                nc.scalar.activation(out=T["e", i][:, c0:c1], in_=T["a", i][:, c0:c1], func=ACT.Sigmoid)

            def ramp_wide(i, c0, c1):
                r = T["r", i][:, c0:c1]
                nc.gpsimd.tensor_tensor(out=r, in0=T["a", i][:, c0:c1], in1=r, op=ALU.subtract)

            def total_wide(i, c0, c1):
                r = T["r", i][:, c0:c1]
                nc.gpsimd.tensor_tensor(out=r, in0=r, in1=T["e", i][:, c0:c1], op=ALU.subtract)
                nc.sync.dma_start(out=rec_v[:, i, c0:c1], in_=r)

            def log(i, c0, c1):
                e = T["e", i][:, c0:c1]
                nc.scalar.activation(out=e, in_=e, func=ACT.Ln, bias=LN_FLOOR)

            def total(i, c0, c1):
                r = T["r", i][:, c0:c1]
                nc.vector.scalar_tensor_tensor(
                    out=r, in0=T["e", i][:, c0:c1], scalar=-CLIP, in1=r, op0=ALU.max, op1=ALU.subtract, reverse1=True
                )
                nc.sync.dma_start(out=rec_v[:, i, c0:c1], in_=r)

            def in_range(i):
                return 0 <= i < TILES

            def z_begin(i):
                stage1(i, "wm", "mu", 1)
                sq_mu(i)
                noise(i)
                sample(i)
                gain(i)

            def z_end(i):
                turn_z(i)
                empty_z(i, "s")
                quant_z(i)

            def head(n):
                if in_range(n):
                    std(n)
                    sum_lv(n)
                if in_range(n + 2):
                    turn_h(n + 2)
                    empty_h(n + 2, "s")
                if in_range(n + 1):
                    quant_h(n + 1)
                    stage1(n + 1, "wl", "acc", 5)
                if in_range(n):
                    red_lv(n)
                if n in {2: 0, 4: 1}:
                    z_begin({2: 0, 4: 1}[n])
                if n - 1 in {2: 0, 4: 1}:
                    z_end({2: 0, 4: 1}[n - 1])
                if in_range(n + 3):
                    widen(n + 3, 0, 8, "v")

            for n in range(-3, TILES):
                head(n)
            if TILES - 1 in {2: 0, 4: 1}:
                z_end({2: 0, 4: 1}[TILES - 1])

            warm = keep.tile([P, 1], F32, name="warm")
            nc.scalar.activation(out=warm[:], in_=s_lv[:, 0:1], func=ACT.Sigmoid)
            for i in range(TILES):
                for c in range(4):
                    stage2(i, c)
                    expo(i, c)
                    x_logit(i, c)
                    if c:
                        ramp(i, c - 1)
                    if c == 0 and in_range(i + 2):
                        z_begin(i + 2)
                ramp(i, 3)
                for b in BATCHES.get(i, ()):
                    for c0 in (0, 1024):
                        log(b, c0, c0 + 1024)
                        total(b, c0, c0 + 1024)
                if in_range(i + 2):
                    z_end(i + 2)
                sq_s(i)

            nc.vector.tensor_tensor(out=kl_a[:], in0=s_mu[:], in1=s_e[:], op=ALU.add)
            nc.vector.tensor_tensor(out=kl_b[:], in0=kl_a[:], in1=s_lv[:], op=ALU.subtract)
            nc.vector.tensor_scalar(
                out=kl_c[:], in0=kl_b[:], scalar1=0.5 / L, scalar2=-0.5, op0=ALU.mult, op1=ALU.add
            )
            nc.sync.dma_start(out=kl.rearrange("(p i) -> p i", i=TILES), in_=kl_c[:])
